import numpy as np
import ml_dtypes


def mxq(x, axis, fmt="e4m3"):
    dtype, down = {"e4m3": (ml_dtypes.float8_e4m3fn, 7), "e5m2": (ml_dtypes.float8_e5m2, 14)}[fmt]
    v = np.moveaxis(np.asarray(x, np.float32).astype(ml_dtypes.bfloat16).astype(np.float64), axis, -1)
    blocks = v.reshape(v.shape[:-1] + (-1, 32))
    amax = np.abs(blocks).max(-1, keepdims=True)
    byte = np.maximum(np.where(amax > 0, np.frexp(amax)[1] - 1 + 127, 0) - down, 1)
    scale = np.exp2(byte - 127.0)
    codes = (blocks / scale).astype(np.float32).astype(dtype).astype(np.float64)
    return np.moveaxis((codes * scale).reshape(v.shape), -1, axis)


WIDE = False


def mx_kscale(k):
    if not WIDE:
        return np.ones(k)
    levels = np.array([10, -10, 5, -5, 0])
    if k % 512:
        return np.exp2(np.random.permutation(np.resize(levels, k // 32))).repeat(32)
    a = np.empty((k // 512, 16))
    for p in range(k // 512):
        a[p, :8] = np.random.permutation(np.resize(levels, 8))
        for g in range(8):
            far = levels[np.abs(levels - a[p, g]) >= 10]
            a[p, g + 8] = far[np.random.randint(len(far))]
    return np.exp2(a.ravel()).repeat(32)


def f64(x):
    return np.asarray(x).astype(np.float64)


def striped(idx):
    return np.tile(idx.reshape(-1, 16).T, (8, 1)).astype(np.uint16)


def unstriped(offs):
    return offs[:16].T.reshape(-1).astype(np.int64)


def striped8(idx):
    return np.concatenate([x.reshape(-1, 16).T for x in idx]).astype(np.uint16)


def runs(offs, k):
    lists = np.stack([offs[16 * r : 16 * r + 16].T.reshape(-1) for r in range(8)]).astype(np.int64)
    return lists[np.arange(k) % 512 // 64]


def pack_weight(w):
    k, n = w.shape
    w = f64(np.asarray(w, np.float32).astype(ml_dtypes.bfloat16)).reshape(k // 32, 32, n)
    amax = np.abs(w).max(1)
    byte = np.clip(np.where(amax > 0, np.frexp(amax)[1] - 1 + 127 - 7, 1), 1, 254)
    scaled = (w * np.exp2(127.0 - byte)[:, None, :]).reshape(k, n).astype(np.float32)
    words = np.ascontiguousarray(scaled.reshape(k // 512, 128, 4, n).transpose(0, 1, 3, 2)).astype(ml_dtypes.float8_e4m3fn).view(np.uint8)
    return words, np.ascontiguousarray(byte.astype(np.uint8).reshape(k // 512, 16, n))


def unpack_weight(words, scales):
    g, p, n, _ = words.shape
    vals = np.ascontiguousarray(words).view(ml_dtypes.float8_e4m3fn).astype(np.float64) * np.repeat(np.exp2(scales.astype(np.float64) - 127.0), 8, axis=1)[..., None]
    return vals.transpose(0, 1, 3, 2).reshape(g * 512, n)


E2M1 = np.array([0.0, 0.5, 1.0, 1.5, 2.0, 3.0, 4.0, 6.0, -0.0, -0.5, -1.0, -1.5, -2.0, -3.0, -4.0, -6.0])


def pack_fp4(w):
    k, n = w.shape
    w = f64(np.asarray(w, np.float32).astype(ml_dtypes.bfloat16)).reshape(k // 32, 32, n)
    amax = np.abs(w).max(1)
    mant, ex = np.frexp(amax / 6.0)
    byte = np.clip(np.where(amax > 0, np.where(mant > 0.5, ex, ex - 1) + 127, 1), 1, 254)
    scaled = (w * np.exp2(127.0 - byte)[:, None, :]).reshape(k, n).astype(np.float32)
    c = np.ascontiguousarray(scaled.reshape(k // 512, 128, 4, n).transpose(0, 1, 3, 2)).astype(ml_dtypes.float4_e2m1fn).view(np.uint8) & 0xF
    words = (c[..., 0::2] | (c[..., 1::2] << 4)).reshape(k // 512, 128, 2 * n)
    return np.ascontiguousarray(words), np.ascontiguousarray(byte.astype(np.uint8).reshape(k // 512, 16, n))


def unpack_fp4(words, scales):
    g, _, n = scales.shape
    words = np.ascontiguousarray(words).reshape(g, 128, n, 2)
    nib = np.empty((g, 128, n, 4), np.uint8)
    nib[..., 0::2] = words & 0xF
    nib[..., 1::2] = words >> 4
    vals = E2M1[nib] * np.repeat(np.exp2(scales.astype(np.float64) - 127.0), 8, axis=1)[..., None]
    return vals.transpose(0, 1, 3, 2).reshape(g * 512, n)


def planes(y):
    n, m = y.shape
    v = y.astype(np.float32).astype(ml_dtypes.bfloat16).astype(np.float64).reshape(n // 32, 32, m)
    top = np.abs(v).max(1)
    byte = np.clip(np.where(top > 0, np.frexp(top)[1] - 1 + 127 - 7, 1), 1, 254)
    codes = (v * np.exp2(127.0 - byte)[:, None, :]).reshape(n, m).astype(np.float32).astype(ml_dtypes.float8_e4m3fn).view(np.uint8)
    words = codes.reshape(n // 512, 128, 4, m).transpose(0, 1, 3, 2)
    return np.ascontiguousarray(words), np.ascontiguousarray(byte.astype(np.uint8).reshape(n // 512, 16, m))


K, T, S, V, N, H = 512, 2048, 512, 256, 512, 512


def setup_inputs():
    n = np.random.standard_normal
    s = mx_kscale(K)[:, None]
    u = mx_kscale(H)
    packed_xT = pack_weight(n((K, T)) * s)
    packed_w1 = pack_fp4(n((K, H)) / np.sqrt(K) / s)
    packed_w2 = pack_fp4(n((H, N)) / np.sqrt(H) / u[:, None])
    return {
        "x_words": packed_xT[0],
        "x_scales": packed_xT[1],
        "w1_words": packed_w1[0],
        "w1_scales": packed_w1[1],
        "rest": np.random.uniform(0.2, 1.0, (H, V)).astype(np.float32),
        "gn": (np.random.uniform(0.5, 1.5, (H, 1)) * u[:, None]).astype(np.float32),
        "w2_words": packed_w2[0],
        "w2_scales": packed_w2[1],
        "offs": striped(np.random.permutation(T)[:S]),
        "a_l": striped8(np.stack([np.random.permutation(S)[:V] for _ in range(8)])),
        "b_l": striped8(np.stack([np.random.permutation(S)[:V] for _ in range(8)])),
    }


def reference(x_words, x_scales, w1_words, w1_scales, rest, gn, w2_words, w2_scales, offs, a_l, b_l):
    xq = unpack_weight(x_words, x_scales)[:, unstriped(offs)]
    y = unpack_fp4(w1_words, w1_scales).T @ xq
    d = y[np.arange(H)[:, None], runs(a_l, H)] - (y[np.arange(H)[:, None], runs(b_l, H)])
    z = f64(gn) * (d * (-1.0 * (f64(rest) / (np.abs(d) + 0.25)) + 1))
    out_0 = unpack_fp4(w2_words, w2_scales).T @ mxq(z, 0, "e4m3")
    return (out_0,) + planes(out_0)

@@ -1,0 +1,184 @@
+from contextlib import ExitStack
+
+import concourse.mybir as mybir
+
+K, T, S, V, N, H = 512, 2048, 512, 256, 512, 512
+FLOPS = 2 * K * H * S + 2 * H * N * V
+
+F32 = mybir.dt.float32
+BF16 = mybir.dt.bfloat16
+I32 = mybir.dt.int32
+U32 = mybir.dt.uint32
+U16 = mybir.dt.uint16
+U8 = mybir.dt.uint8
+FP8X4 = mybir.dt.float8_e4m3fn_x4
+FP4X4 = mybir.dt.float4_e2m1fn_x4
+ALU = mybir.AluOpType
+ACT = mybir.ActivationFunctionType
+
+P = 128
+PACK = 4
+LIST = 16
+S_PART = 256
+V_PART = 128
+
+
+def load_scale_rows(queue, tile, scales, q):
+    queue.dma_start(
+        out=tile[:].bitcast(I32)[32 * q : 32 * q + 4, :], in_=scales[0].bitcast(I32)[4 * q : 4 * q + 4, :]
+    )
+
+
+def deal_words(nc, dealt, raw):
+    nc.vector.tensor_copy(
+        out=dealt[:].rearrange("p (t m e) -> p t m e", t=PACK, e=2),
+        in_=raw[:].rearrange("p (m t e) -> p t m e", t=PACK, e=2),
+    )
+
+
+def deal_scales(nc, dealt, raw):
+    nc.vector.tensor_copy(
+        out=dealt[:].rearrange("p (t m) -> p t m", t=PACK),
+        in_=raw[:].rearrange("p (m t) -> p t m", t=PACK),
+    )
+
+
+def tile_picked_restlen_none_po_kernel(
+    tc, x_words, x_scales, w1_words, w1_scales, rest, gn, w2_words, w2_scales, offs, a_l, b_l, out_0, out_1, out_2
+):
+    nc = tc.nc
+    with ExitStack() as ctx:
+        keep = ctx.enter_context(tc.tile_pool(name="keep", bufs=1))
+        psum = ctx.enter_context(tc.psum_pool(name="psum", bufs=8))
+
+        offs_t = keep.tile([P, S // LIST], U16, name="offs_t")
+        a_t = keep.tile([P, V // LIST], U16, name="a_t")
+        b_t = keep.tile([P, V // LIST], U16, name="b_t")
+        xw = keep.tile([P, T], U32, name="xw", align_bytes=64)
+        xs = keep.tile([P, T], U8, name="xs", tag="xs_rest", align_bytes=64)
+        w1_raw = keep.tile([P, 2 * H], U8, name="w1_raw", tag="w_raw", align_bytes=64)
+        ws_raw = keep.tile([P, H], U8, name="ws_raw", align_bytes=64)
+        gn_t = keep.tile([P, PACK], F32, name="gn_t")
+        warm_in = keep.tile([P, 1], F32, name="warm_in")
+        warm_out = keep.tile([P, 1], F32, name="warm_out")
+
+        nc.gpsimd.memset(ws_raw[:].bitcast(I32), 0)
+        nc.vector.memset(xs[:].bitcast(I32), 0)
+        nc.vector.memset(warm_in[:], 1.0)
+        nc.sync.dma_start(offs_t[:], offs)
+        nc.scalar.dma_start(out=w1_raw[:].bitcast(I32), in_=w1_words[0].bitcast(I32))
+        nc.sync.dma_start(a_t[:], a_l)
+        nc.sync.dma_start(out=xw[:].bitcast(I32), in_=x_words[0].rearrange("p c r -> p (c r)").bitcast(I32))
+        nc.sync.dma_start(b_t[:], b_l)
+        for q in range(4):
+            load_scale_rows(nc.scalar, xs, x_scales, q)
+        for q in range(4):
+            load_scale_rows(nc.gpsimd if q < 2 else nc.scalar, ws_raw, w1_scales, q)
+        nc.scalar.activation(warm_out[:], warm_in[:], ACT.Abs_reciprocal_sqrt)
+        nc.gpsimd.dma_start(out=gn_t[:], in_=gn.rearrange("(p t) o -> p (t o)", t=PACK))
+
+        w1 = keep.tile([P, 2 * H], U8, name="w1", align_bytes=64)
+        w1s = keep.tile([P, H], U8, name="w1s", align_bytes=64)
+        deal_words(nc, w1, w1_raw)
+        w2_raw = keep.tile([P, 2 * N], U8, name="w2_raw", tag="w_raw", align_bytes=64)
+        nc.sync.dma_start(out=w2_raw[:].bitcast(I32), in_=w2_words[0].bitcast(I32))
+
+        xgs = keep.tile([P, S], U8, name="xgs", align_bytes=64)
+        nc.vector.tensor_copy(xgs[:], xs[:].indirect(offs_t[:]))
+        rest_t = keep.tile([P, PACK, V], F32, name="rest_t", tag="xs_rest", align_bytes=64)
+        nc.sync.dma_start(out=rest_t[:], in_=rest.rearrange("(p t) v -> p t v", t=PACK))
+        deal_scales(nc, w1s, ws_raw)
+        for q in range(4):
+            load_scale_rows(nc.sync, ws_raw, w2_scales, q)
+
+        y = [keep.tile([P, S], F32, name=f"y{t}", align_bytes=64) for t in range(PACK)]
+        for s0 in range(0, S, S_PART):
+            xg = keep.tile([P, S_PART], U32, name=f"xg{s0}", align_bytes=64)
+            nc.vector.tensor_copy(xg[:], xw[:].indirect(offs_t[:, s0 // LIST : (s0 + S_PART) // LIST]))
+            for t in range(PACK):
+                acc = psum.tile([P, S_PART], F32, name="acc", tag="bank")
+                nc.tensor.matmul_mx(
+                    out=acc[:],
+                    lhsT=w1[:, 2 * P * t : 2 * P * (t + 1)].bitcast(FP4X4),
+                    lhsT_scale=w1s[:, P * t : P * (t + 1)],
+                    rhs=xg[:].bitcast(FP8X4),
+                    rhs_scale=xgs[:, s0 : s0 + S_PART],
+                    start=True,
+                    stop=True,
+                )
+                nc.scalar.copy(y[t][:, s0 : s0 + S_PART], acc[:])
+
+        w2 = keep.tile([P, 2 * N], U8, name="w2", align_bytes=64)
+        w2s = keep.tile([P, N], U8, name="w2s", align_bytes=64)
+        deal_words(nc, w2, w2_raw)
+        deal_scales(nc, w2s, ws_raw)
+
+        parts = range(0, V, V_PART)
+        nd = {}
+        r = {}
+        for v0 in parts:
+            cols = slice(v0 // LIST, (v0 + V_PART) // LIST)
+            ya = keep.tile([P, PACK, V_PART], F32, name=f"ya{v0}", align_bytes=64)
+            nd[v0] = keep.tile([P, PACK, V_PART], F32, name=f"nd{v0}", align_bytes=64)
+            for t in range(PACK):
+                nc.vector.tensor_copy(ya[:, t, :], y[t][:].indirect(a_t[:, cols]))
+            for t in range(PACK):
+                nc.vector.tensor_tensor(nd[v0][:, t, :], y[t][:].indirect(b_t[:, cols]), ya[:, t, :], ALU.subtract)
+            mag = keep.tile([P, PACK, V_PART], F32, name=f"mag{v0}", align_bytes=64)
+            sq = keep.tile([P, PACK, V_PART], F32, name=f"sq{v0}", align_bytes=64)
+            r[v0] = keep.tile([P, PACK, V_PART], F32, name=f"r{v0}", align_bytes=64)
+            nc.scalar.activation(mag[:], nd[v0][:], ACT.Abs)
+            nc.scalar.activation(sq[:], mag[:], ACT.Square, bias=0.25)
+            nc.scalar.activation(r[v0][:], sq[:], ACT.Abs_reciprocal_sqrt)
+
+        out_rows = out_0.rearrange("(p t) v -> p t v", t=PACK)
+        out_words = out_1[0].rearrange("p c r -> p (c r)").bitcast(I32)
+        oc = keep.tile([P, V], U32, name="oc", align_bytes=64)
+        osc = keep.tile([P, V], U8, name="osc", align_bytes=64)
+        o32 = {}
+        for v0 in parts:
+            pull = keep.tile([P, PACK, V_PART], F32, name=f"pull{v0}", align_bytes=64)
+            zb = keep.tile([P, PACK, V_PART], BF16, name=f"zb{v0}", align_bytes=64)
+            zi = keep.tile([P, V_PART, PACK], BF16, name=f"zi{v0}", align_bytes=64)
+            zc = keep.tile([P, V_PART], U32, name=f"zc{v0}", align_bytes=64)
+            zs = keep.tile([P, V_PART], U8, name=f"zs{v0}", align_bytes=64)
+            for t in range(PACK):
+                nc.vector.scalar_tensor_tensor(
+                    pull[:, t, :], r[v0][:, t, :], gn_t[:, t : t + 1], rest_t[:, t, v0 : v0 + V_PART], ALU.mult, ALU.mult
+                )
+            for t in range(PACK):
+                nc.vector.scalar_tensor_tensor(
+                    zb[:, t, :], pull[:, t, :], gn_t[:, t : t + 1], nd[v0][:, t, :], ALU.subtract, ALU.mult
+                )
+            nc.vector.tensor_copy(out=zi[:], in_=zb[:].rearrange("p t v -> p v t"))
+            nc.vector.quantize_mx(out=zc[:].bitcast(FP8X4), scales=zs[:], in_=zi[:].rearrange("p v t -> p (v t)"))
+            o32[v0] = keep.tile([P, PACK, V_PART], F32, name=f"o32{v0}", align_bytes=64)
+            per_bank = 512 // V_PART
+            for t0 in range(0, PACK, per_bank):
+                res = psum.tile([P, per_bank, V_PART], F32, name="res", tag="bank")
+                for t in range(t0, t0 + per_bank):
+                    nc.tensor.matmul_mx(
+                        out=res[:, t - t0, :],
+                        lhsT=w2[:, 2 * P * t : 2 * P * (t + 1)].bitcast(FP4X4),
+                        lhsT_scale=w2s[:, P * t : P * (t + 1)],
+                        rhs=zc[:].bitcast(FP8X4),
+                        rhs_scale=zs[:],
+                        start=True,
+                        stop=True,
+                    )
+                nc.scalar.copy(o32[v0][:, t0 : t0 + per_bank, :], res[:])
+            nc.sync.dma_start(out=out_rows[:, :, v0 : v0 + V_PART], in_=o32[v0][:])
+        for v0 in parts:
+            oi = keep.tile([P, V_PART, PACK], BF16, name=f"oi{v0}", align_bytes=64)
+            nc.vector.tensor_copy(out=oi[:], in_=o32[v0][:].rearrange("p t v -> p v t"))
+            nc.vector.quantize_mx(
+                out=oc[:, v0 : v0 + V_PART].bitcast(FP8X4),
+                scales=osc[:, v0 : v0 + V_PART],
+                in_=oi[:].rearrange("p v t -> p (v t)"),
+            )
+            nc.sync.dma_start(out=out_words[:, v0 : v0 + V_PART], in_=oc[:, v0 : v0 + V_PART].bitcast(I32))
+        for q in range(4):
+            queue = nc.scalar if q % 2 else nc.sync
+            queue.dma_start(
+                out=out_2[0].bitcast(I32)[4 * q : 4 * q + 4, :], in_=osc[:].bitcast(I32)[32 * q : 32 * q + 4, :]
+            )

@@ -32,14 +32,14 @@ def load_scale_rows(queue, tile, scales, q):
 def deal_words(nc, dealt, raw):
     nc.vector.tensor_copy(
         out=dealt[:].rearrange("p (t m e) -> p t m e", t=PACK, e=2),
-        in_=raw[:].rearrange("p (m t e) -> p t m e", t=PACK, e=2),
+        in_=raw.rearrange("p (m t e) -> p t m e", t=PACK, e=2),
     )
 
 
 def deal_scales(nc, dealt, raw):
     nc.vector.tensor_copy(
         out=dealt[:].rearrange("p (t m) -> p t m", t=PACK),
-        in_=raw[:].rearrange("p (m t) -> p t m", t=PACK),
+        in_=raw.rearrange("p (m t) -> p t m", t=PACK),
     )
 
 
@@ -58,50 +58,54 @@ def tile_picked_restlen_none_po_kernel(
         xs = keep.tile([P, T], U8, name="xs", tag="xs_rest", align_bytes=64)
         w1_raw = keep.tile([P, 2 * H], U8, name="w1_raw", tag="w_raw", align_bytes=64)
         ws_raw = keep.tile([P, H], U8, name="ws_raw", align_bytes=64)
-        gn_t = keep.tile([P, PACK], F32, name="gn_t")
-        warm_in = keep.tile([P, 1], F32, name="warm_in")
+        warm_in = keep.tile([P, 1], F32, name="warm_in", tag="warm")
         warm_out = keep.tile([P, 1], F32, name="warm_out")
 
-        nc.gpsimd.memset(ws_raw[:].bitcast(I32), 0)
-        nc.vector.memset(xs[:].bitcast(I32), 0)
+        nc.gpsimd.memset(xs[:].bitcast(I32), 0)
         nc.vector.memset(warm_in[:], 1.0)
         nc.sync.dma_start(offs_t[:], offs)
-        nc.scalar.dma_start(out=w1_raw[:].bitcast(I32), in_=w1_words[0].bitcast(I32))
+        nc.scalar.dma_start(out=xw[:].bitcast(I32), in_=x_words[0].rearrange("p c r -> p (c r)").bitcast(I32))
+        nc.sync.dma_start(out=w1_raw[:].bitcast(I32), in_=w1_words[0].bitcast(I32))
+        w1s_rows = w1_scales[0].bitcast(I32)
+        nc.sync.dma_start(out=ws_raw[:].bitcast(I32)[0:98, :], in_=w1s_rows[0:14, :].partition_broadcast(7))
+        for q in range(4):
+            load_scale_rows(nc.sync, xs, x_scales, q)
+        nc.gpsimd.dma_start(out=ws_raw[:].bitcast(I32)[98:128, :], in_=w1s_rows[14:16, :].partition_broadcast(15))
         nc.sync.dma_start(a_t[:], a_l)
-        nc.sync.dma_start(out=xw[:].bitcast(I32), in_=x_words[0].rearrange("p c r -> p (c r)").bitcast(I32))
         nc.sync.dma_start(b_t[:], b_l)
-        for q in range(4):
-            load_scale_rows(nc.scalar, xs, x_scales, q)
-        for q in range(4):
-            load_scale_rows(nc.gpsimd if q < 2 else nc.scalar, ws_raw, w1_scales, q)
         nc.scalar.activation(warm_out[:], warm_in[:], ACT.Abs_reciprocal_sqrt)
-        nc.gpsimd.dma_start(out=gn_t[:], in_=gn.rearrange("(p t) o -> p (t o)", t=PACK))
 
         w1 = keep.tile([P, 2 * H], U8, name="w1", align_bytes=64)
         w1s = keep.tile([P, H], U8, name="w1s", align_bytes=64)
-        deal_words(nc, w1, w1_raw)
-        w2_raw = keep.tile([P, 2 * N], U8, name="w2_raw", tag="w_raw", align_bytes=64)
-        nc.sync.dma_start(out=w2_raw[:].bitcast(I32), in_=w2_words[0].bitcast(I32))
+        deal_words(nc, w1, w1_raw[:])
+        w2_raw = keep.tile([P, 3 * N], U8, name="w2_raw", tag="w_raw", align_bytes=64)
+        w2_dst = w2_raw[:].bitcast(I32)
+        w2s_rows = w2_scales[0].bitcast(I32)
+        nc.scalar.dma_start(out=w2_dst[:, : N // 2], in_=w2_words[0].bitcast(I32))
+        nc.scalar.dma_start(out=w2_dst[0:98, N // 2 :], in_=w2s_rows[0:14, :].partition_broadcast(7))
+        nc.scalar.dma_start(out=w2_dst[98:128, N // 2 :], in_=w2s_rows[14:16, :].partition_broadcast(15))
 
         xgs = keep.tile([P, S], U8, name="xgs", align_bytes=64)
         nc.vector.tensor_copy(xgs[:], xs[:].indirect(offs_t[:]))
         rest_t = keep.tile([P, PACK, V], F32, name="rest_t", tag="xs_rest", align_bytes=64)
         nc.sync.dma_start(out=rest_t[:], in_=rest.rearrange("(p t) v -> p t v", t=PACK))
-        deal_scales(nc, w1s, ws_raw)
-        for q in range(4):
-            load_scale_rows(nc.sync, ws_raw, w2_scales, q)
+        deal_scales(nc, w1s, ws_raw[:])
+        gn_t = keep.tile([P, PACK], F32, name="gn_t", tag="warm")
+        nc.sync.dma_start(out=gn_t[:], in_=gn.rearrange("(p t) o -> p (t o)", t=PACK))
 
         y = [keep.tile([P, S], F32, name=f"y{t}", align_bytes=64) for t in range(PACK)]
+        xg = {}
         for s0 in range(0, S, S_PART):
-            xg = keep.tile([P, S_PART], U32, name=f"xg{s0}", align_bytes=64)
-            nc.vector.tensor_copy(xg[:], xw[:].indirect(offs_t[:, s0 // LIST : (s0 + S_PART) // LIST]))
-            for t in range(PACK):
+            xg[s0] = keep.tile([P, S_PART], U32, name=f"xg{s0}", align_bytes=64)
+            nc.vector.tensor_copy(xg[s0][:], xw[:].indirect(offs_t[:, s0 // LIST : (s0 + S_PART) // LIST]))
+        for t in range(PACK):
+            for s0 in range(0, S, S_PART):
                 acc = psum.tile([P, S_PART], F32, name="acc", tag="bank")
                 nc.tensor.matmul_mx(
                     out=acc[:],
                     lhsT=w1[:, 2 * P * t : 2 * P * (t + 1)].bitcast(FP4X4),
                     lhsT_scale=w1s[:, P * t : P * (t + 1)],
-                    rhs=xg[:].bitcast(FP8X4),
+                    rhs=xg[s0][:].bitcast(FP8X4),
                     rhs_scale=xgs[:, s0 : s0 + S_PART],
                     start=True,
                     stop=True,
@@ -110,53 +114,76 @@ def tile_picked_restlen_none_po_kernel(
 
         w2 = keep.tile([P, 2 * N], U8, name="w2", align_bytes=64)
         w2s = keep.tile([P, N], U8, name="w2s", align_bytes=64)
-        deal_words(nc, w2, w2_raw)
-        deal_scales(nc, w2s, ws_raw)
+        deal_words(nc, w2, w2_raw[:, : 2 * N])
+        deal_scales(nc, w2s, w2_raw[:, 2 * N :])
 
         parts = range(0, V, V_PART)
+        groups = [(0, 0, V)] + [(2, v0, V_PART) for v0 in parts]
+        ya = {}
         nd = {}
         r = {}
-        for v0 in parts:
-            cols = slice(v0 // LIST, (v0 + V_PART) // LIST)
-            ya = keep.tile([P, PACK, V_PART], F32, name=f"ya{v0}", align_bytes=64)
-            nd[v0] = keep.tile([P, PACK, V_PART], F32, name=f"nd{v0}", align_bytes=64)
-            for t in range(PACK):
-                nc.vector.tensor_copy(ya[:, t, :], y[t][:].indirect(a_t[:, cols]))
-            for t in range(PACK):
-                nc.vector.tensor_tensor(nd[v0][:, t, :], y[t][:].indirect(b_t[:, cols]), ya[:, t, :], ALU.subtract)
-            mag = keep.tile([P, PACK, V_PART], F32, name=f"mag{v0}", align_bytes=64)
-            sq = keep.tile([P, PACK, V_PART], F32, name=f"sq{v0}", align_bytes=64)
-            r[v0] = keep.tile([P, PACK, V_PART], F32, name=f"r{v0}", align_bytes=64)
-            nc.scalar.activation(mag[:], nd[v0][:], ACT.Abs)
+        for g in groups:
+            t0, v0, width = g
+            if v0 == 0:
+                for t in (t0, t0 + 1):
+                    ya[t] = keep.tile([P, V], F32, name=f"ya{t}", align_bytes=64)
+                    nc.vector.tensor_copy(ya[t][:], y[t][:].indirect(a_t[:]))
+            name = f"{t0}_{v0}"
+            nd[g] = keep.tile([P, 2, width], F32, name=f"nd{name}", align_bytes=64)
+            for i in range(2):
+                nc.vector.tensor_tensor(
+                    nd[g][:, i, :],
+                    y[t0 + i][:].indirect(b_t[:, v0 // LIST : (v0 + width) // LIST]),
+                    ya[t0 + i][:, v0 : v0 + width],
+                    ALU.subtract,
+                )
+            mag = keep.tile([P, 2, width], F32, name=f"mag{name}", align_bytes=64)
+            sq = keep.tile([P, 2, width], F32, name=f"sq{name}", align_bytes=64)
+            r[g] = keep.tile([P, 2, width], F32, name=f"r{name}", align_bytes=64)
+            nc.scalar.activation(mag[:], nd[g][:], ACT.Abs)
             nc.scalar.activation(sq[:], mag[:], ACT.Square, bias=0.25)
-            nc.scalar.activation(r[v0][:], sq[:], ACT.Abs_reciprocal_sqrt)
+            nc.scalar.activation(r[g][:], sq[:], ACT.Abs_reciprocal_sqrt)
 
         out_rows = out_0.rearrange("(p t) v -> p t v", t=PACK)
         out_words = out_1[0].rearrange("p c r -> p (c r)").bitcast(I32)
         oc = keep.tile([P, V], U32, name="oc", align_bytes=64)
         osc = keep.tile([P, V], U8, name="osc", align_bytes=64)
+        zb = {v0: keep.tile([P, PACK, V_PART], BF16, name=f"zb{v0}", align_bytes=64) for v0 in parts}
         o32 = {}
-        for v0 in parts:
-            pull = keep.tile([P, PACK, V_PART], F32, name=f"pull{v0}", align_bytes=64)
-            zb = keep.tile([P, PACK, V_PART], BF16, name=f"zb{v0}", align_bytes=64)
+
+        def force(g):
+            t0, v0, width = g
+            pull = keep.tile([P, 2, width], F32, name=f"pull{t0}_{v0}", align_bytes=64)
+            for i in range(2):
+                t = t0 + i
+                nc.vector.scalar_tensor_tensor(
+                    pull[:, i, :], r[g][:, i, :], gn_t[:, t : t + 1], rest_t[:, t, v0 : v0 + width], ALU.mult, ALU.mult
+                )
+            for c0 in range(0, width, V_PART):
+                for i in range(2):
+                    t = t0 + i
+                    nc.vector.scalar_tensor_tensor(
+                        zb[v0 + c0][:, t, :],
+                        pull[:, i, c0 : c0 + V_PART],
+                        gn_t[:, t : t + 1],
+                        nd[g][:, i, c0 : c0 + V_PART],
+                        ALU.subtract,
+                        ALU.mult,
+                    )
+
+        force(groups[0])
+        for g in groups[1:]:
+            v0 = g[1]
+            force(g)
             zi = keep.tile([P, V_PART, PACK], BF16, name=f"zi{v0}", align_bytes=64)
             zc = keep.tile([P, V_PART], U32, name=f"zc{v0}", align_bytes=64)
             zs = keep.tile([P, V_PART], U8, name=f"zs{v0}", align_bytes=64)
-            for t in range(PACK):
-                nc.vector.scalar_tensor_tensor(
-                    pull[:, t, :], r[v0][:, t, :], gn_t[:, t : t + 1], rest_t[:, t, v0 : v0 + V_PART], ALU.mult, ALU.mult
-                )
-            for t in range(PACK):
-                nc.vector.scalar_tensor_tensor(
-                    zb[:, t, :], pull[:, t, :], gn_t[:, t : t + 1], nd[v0][:, t, :], ALU.subtract, ALU.mult
-                )
-            nc.vector.tensor_copy(out=zi[:], in_=zb[:].rearrange("p t v -> p v t"))
+            nc.vector.tensor_copy(out=zi[:], in_=zb[v0][:].rearrange("p t v -> p v t"))
             nc.vector.quantize_mx(out=zc[:].bitcast(FP8X4), scales=zs[:], in_=zi[:].rearrange("p v t -> p (v t)"))
             o32[v0] = keep.tile([P, PACK, V_PART], F32, name=f"o32{v0}", align_bytes=64)
-            per_bank = 512 // V_PART
-            for t0 in range(0, PACK, per_bank):
-                res = psum.tile([P, per_bank, V_PART], F32, name="res", tag="bank")
-                for t in range(t0, t0 + per_bank):
+            for t0 in range(0, PACK, 2):
+                res = psum.tile([P, 2, V_PART], F32, name="res", tag="bank")
+                for t in (t0, t0 + 1):
                     nc.tensor.matmul_mx(
                         out=res[:, t - t0, :],
                         lhsT=w2[:, 2 * P * t : 2 * P * (t + 1)].bitcast(FP4X4),
@@ -166,7 +193,7 @@ def tile_picked_restlen_none_po_kernel(
                         start=True,
                         stop=True,
                     )
-                nc.scalar.copy(o32[v0][:, t0 : t0 + per_bank, :], res[:])
+                nc.scalar.copy(o32[v0][:, t0 : t0 + 2, :], res[:])
             nc.sync.dma_start(out=out_rows[:, :, v0 : v0 + V_PART], in_=o32[v0][:])
         for v0 in parts:
             oi = keep.tile([P, V_PART, PACK], BF16, name=f"oi{v0}", align_bytes=64)

@@ -118,31 +118,37 @@ def tile_picked_restlen_none_po_kernel(
         deal_scales(nc, w2s, w2_raw[:, 2 * N :])
 
         parts = range(0, V, V_PART)
-        groups = [(0, 0, V)] + [(2, v0, V_PART) for v0 in parts]
-        ya = {}
+        waves = [[(0, 0, V), (1, 0, V)], [(2, 0, V)] + [(3, v0, V_PART) for v0 in parts]]
         nd = {}
         r = {}
-        for g in groups:
-            t0, v0, width = g
-            if v0 == 0:
-                for t in (t0, t0 + 1):
-                    ya[t] = keep.tile([P, V], F32, name=f"ya{t}", align_bytes=64)
-                    nc.vector.tensor_copy(ya[t][:], y[t][:].indirect(a_t[:]))
-            name = f"{t0}_{v0}"
-            nd[g] = keep.tile([P, 2, width], F32, name=f"nd{name}", align_bytes=64)
-            for i in range(2):
+        for wave in waves:
+            ya = {}
+            for t in sorted(set(piece[0] for piece in wave)):
+                ya[t] = keep.tile([P, V], F32, name=f"ya{t}", align_bytes=64)
+                nc.vector.tensor_copy(ya[t][:], y[t][:].indirect(a_t[:]))
+            stages = {}
+            for piece in wave:
+                t, v0, width = piece
+                nd[piece] = keep.tile([P, width], F32, name=f"nd{t}_{v0}", align_bytes=64)
                 nc.vector.tensor_tensor(
-                    nd[g][:, i, :],
-                    y[t0 + i][:].indirect(b_t[:, v0 // LIST : (v0 + width) // LIST]),
-                    ya[t0 + i][:, v0 : v0 + width],
+                    nd[piece][:],
+                    y[t][:].indirect(b_t[:, v0 // LIST : (v0 + width) // LIST]),
+                    ya[t][:, v0 : v0 + width],
                     ALU.subtract,
                 )
-            mag = keep.tile([P, 2, width], F32, name=f"mag{name}", align_bytes=64)
-            sq = keep.tile([P, 2, width], F32, name=f"sq{name}", align_bytes=64)
-            r[g] = keep.tile([P, 2, width], F32, name=f"r{name}", align_bytes=64)
-            nc.scalar.activation(mag[:], nd[g][:], ACT.Abs)
-            nc.scalar.activation(sq[:], mag[:], ACT.Square, bias=0.25)
-            nc.scalar.activation(r[g][:], sq[:], ACT.Abs_reciprocal_sqrt)
+                mag = keep.tile([P, width], F32, name=f"mag{t}_{v0}", align_bytes=64)
+                sq = keep.tile([P, width], F32, name=f"sq{t}_{v0}", align_bytes=64)
+                r[piece] = keep.tile([P, width], F32, name=f"r{t}_{v0}", align_bytes=64)
+                stages[piece] = [
+                    (mag, nd[piece], ACT.Abs, 0.0),
+                    (sq, mag, ACT.Square, 0.25),
+                    (r[piece], sq, ACT.Abs_reciprocal_sqrt, 0.0),
+                ]
+            for step in range(len(wave) + 2):
+                for stage in range(3):
+                    if 0 <= step - stage < len(wave):
+                        dst, src, func, bias = stages[wave[step - stage]][stage]
+                        nc.scalar.activation(dst[:], src[:], func, bias=bias)
 
         out_rows = out_0.rearrange("(p t) v -> p t v", t=PACK)
         out_words = out_1[0].rearrange("p c r -> p (c r)").bitcast(I32)
@@ -151,34 +157,38 @@ def tile_picked_restlen_none_po_kernel(
         zb = {v0: keep.tile([P, PACK, V_PART], BF16, name=f"zb{v0}", align_bytes=64) for v0 in parts}
         o32 = {}
 
-        def force(g):
-            t0, v0, width = g
-            pull = keep.tile([P, 2, width], F32, name=f"pull{t0}_{v0}", align_bytes=64)
-            for i in range(2):
-                t = t0 + i
-                nc.vector.scalar_tensor_tensor(
-                    pull[:, i, :], r[g][:, i, :], gn_t[:, t : t + 1], rest_t[:, t, v0 : v0 + width], ALU.mult, ALU.mult
-                )
-            for c0 in range(0, width, V_PART):
-                for i in range(2):
-                    t = t0 + i
-                    nc.vector.scalar_tensor_tensor(
-                        zb[v0 + c0][:, t, :],
-                        pull[:, i, c0 : c0 + V_PART],
-                        gn_t[:, t : t + 1],
-                        nd[g][:, i, c0 : c0 + V_PART],
-                        ALU.subtract,
-                        ALU.mult,
-                    )
+        pull = {}
 
-        force(groups[0])
-        for g in groups[1:]:
-            v0 = g[1]
-            force(g)
+        def pull_of(piece):
+            t, v0, width = piece
+            pull[piece] = keep.tile([P, width], F32, name=f"pull{t}_{v0}", align_bytes=64)
+            nc.vector.scalar_tensor_tensor(
+                pull[piece][:], r[piece][:], gn_t[:, t : t + 1], rest_t[:, t, v0 : v0 + width], ALU.mult, ALU.mult
+            )
+
+        def force(piece, v0):
+            t, first, width = piece
+            cols = slice(v0 - first, v0 - first + V_PART)
+            nc.vector.scalar_tensor_tensor(
+                zb[v0][:, t, :], pull[piece][:, cols], gn_t[:, t : t + 1], nd[piece][:, cols], ALU.subtract, ALU.mult
+            )
+
+        for piece in waves[0]:
+            pull_of(piece)
+        for v0 in parts:
+            for piece in waves[0]:
+                force(piece, v0)
+        pull_of(waves[1][0])
+        for last in waves[1][1:]:
+            v0 = last[1]
+            pull_of(last)
+            force(waves[1][0], v0)
+            force(last, v0)
             zi = keep.tile([P, V_PART, PACK], BF16, name=f"zi{v0}", align_bytes=64)
             zc = keep.tile([P, V_PART], U32, name=f"zc{v0}", align_bytes=64)
             zs = keep.tile([P, V_PART], U8, name=f"zs{v0}", align_bytes=64)
-            nc.vector.tensor_copy(out=zi[:], in_=zb[v0][:].rearrange("p t v -> p v t"))
+            weave = nc.scalar.copy if v0 == 0 else nc.vector.tensor_copy
+            weave(zi[:], zb[v0][:].rearrange("p t v -> p v t"))
             nc.vector.quantize_mx(out=zc[:].bitcast(FP8X4), scales=zs[:], in_=zi[:].rearrange("p v t -> p (v t)"))
             o32[v0] = keep.tile([P, PACK, V_PART], F32, name=f"o32{v0}", align_bytes=64)
             for t0 in range(0, PACK, 2):

from contextlib import ExitStack

import concourse.mybir as mybir

K, T, S, V, N, H = 512, 2048, 512, 256, 512, 512
FLOPS = 2 * K * H * S + 2 * H * N * V

F32 = mybir.dt.float32
BF16 = mybir.dt.bfloat16
I32 = mybir.dt.int32
U32 = mybir.dt.uint32
U16 = mybir.dt.uint16
U8 = mybir.dt.uint8
FP8X4 = mybir.dt.float8_e4m3fn_x4
FP4X4 = mybir.dt.float4_e2m1fn_x4
ALU = mybir.AluOpType
ACT = mybir.ActivationFunctionType

P = 128
PACK = 4
LIST = 16
S_PART = 256
V_PART = 128


def load_scale_rows(queue, tile, scales, q):
    queue.dma_start(
        out=tile[:].bitcast(I32)[32 * q : 32 * q + 4, :], in_=scales[0].bitcast(I32)[4 * q : 4 * q + 4, :]
    )


def deal_words(nc, dealt, raw):
    nc.vector.tensor_copy(
        out=dealt[:].rearrange("p (t m e) -> p t m e", t=PACK, e=2),
        in_=raw.rearrange("p (m t e) -> p t m e", t=PACK, e=2),
    )


def deal_scales(nc, dealt, raw):
    nc.vector.tensor_copy(
        out=dealt[:].rearrange("p (t m) -> p t m", t=PACK),
        in_=raw.rearrange("p (m t) -> p t m", t=PACK),
    )


def tile_picked_restlen_none_po_kernel(
    tc, x_words, x_scales, w1_words, w1_scales, rest, gn, w2_words, w2_scales, offs, a_l, b_l, out_0, out_1, out_2
):
    nc = tc.nc
    with ExitStack() as ctx:
        keep = ctx.enter_context(tc.tile_pool(name="keep", bufs=1))
        psum = ctx.enter_context(tc.psum_pool(name="psum", bufs=8))

        offs_t = keep.tile([P, S // LIST], U16, name="offs_t")
        a_t = keep.tile([P, V // LIST], U16, name="a_t")
        b_t = keep.tile([P, V // LIST], U16, name="b_t")
        xw = keep.tile([P, T], U32, name="xw", align_bytes=64)
        xs = keep.tile([P, T], U8, name="xs", tag="xs_rest", align_bytes=64)
        w1_raw = keep.tile([P, 2 * H], U8, name="w1_raw", tag="w_raw", align_bytes=64)
        ws_raw = keep.tile([P, H], U8, name="ws_raw", align_bytes=64)
        warm_in = keep.tile([P, 1], F32, name="warm_in", tag="warm")
        warm_out = keep.tile([P, 1], F32, name="warm_out")

        nc.gpsimd.memset(xs[:].bitcast(I32), 0)
        nc.vector.memset(warm_in[:], 1.0)
        nc.sync.dma_start(offs_t[:], offs)
        nc.scalar.dma_start(out=xw[:].bitcast(I32), in_=x_words[0].rearrange("p c r -> p (c r)").bitcast(I32))
        nc.sync.dma_start(out=w1_raw[:].bitcast(I32), in_=w1_words[0].bitcast(I32))
        w1s_rows = w1_scales[0].bitcast(I32)
        nc.sync.dma_start(out=ws_raw[:].bitcast(I32)[0:98, :], in_=w1s_rows[0:14, :].partition_broadcast(7))
        for q in range(4):
            load_scale_rows(nc.sync, xs, x_scales, q)
        nc.gpsimd.dma_start(out=ws_raw[:].bitcast(I32)[98:128, :], in_=w1s_rows[14:16, :].partition_broadcast(15))
        nc.sync.dma_start(a_t[:], a_l)
        nc.sync.dma_start(b_t[:], b_l)
        nc.scalar.activation(warm_out[:], warm_in[:], ACT.Abs_reciprocal_sqrt)

        w1 = keep.tile([P, 2 * H], U8, name="w1", align_bytes=64)
        w1s = keep.tile([P, H], U8, name="w1s", align_bytes=64)
        deal_words(nc, w1, w1_raw[:])
        w2_raw = keep.tile([P, 3 * N], U8, name="w2_raw", tag="w_raw", align_bytes=64)
        w2_dst = w2_raw[:].bitcast(I32)
        w2s_rows = w2_scales[0].bitcast(I32)
        nc.scalar.dma_start(out=w2_dst[:, : N // 2], in_=w2_words[0].bitcast(I32))
        nc.scalar.dma_start(out=w2_dst[0:98, N // 2 :], in_=w2s_rows[0:14, :].partition_broadcast(7))
        nc.scalar.dma_start(out=w2_dst[98:128, N // 2 :], in_=w2s_rows[14:16, :].partition_broadcast(15))

        xgs = keep.tile([P, S], U8, name="xgs", align_bytes=64)
        nc.vector.tensor_copy(xgs[:], xs[:].indirect(offs_t[:]))
        rest_t = keep.tile([P, PACK, V], F32, name="rest_t", tag="xs_rest", align_bytes=64)
        nc.sync.dma_start(out=rest_t[:], in_=rest.rearrange("(p t) v -> p t v", t=PACK))
        deal_scales(nc, w1s, ws_raw[:])
        gn_t = keep.tile([P, PACK], F32, name="gn_t", tag="warm")
        nc.sync.dma_start(out=gn_t[:], in_=gn.rearrange("(p t) o -> p (t o)", t=PACK))

        y = [keep.tile([P, S], F32, name=f"y{t}", align_bytes=64) for t in range(PACK)]
        xg = {}
        for s0 in range(0, S, S_PART):
            xg[s0] = keep.tile([P, S_PART], U32, name=f"xg{s0}", align_bytes=64)
            nc.vector.tensor_copy(xg[s0][:], xw[:].indirect(offs_t[:, s0 // LIST : (s0 + S_PART) // LIST]))
        for t in range(PACK):
            for s0 in range(0, S, S_PART):
                acc = psum.tile([P, S_PART], F32, name="acc", tag="bank")
                nc.tensor.matmul_mx(
                    out=acc[:],
                    lhsT=w1[:, 2 * P * t : 2 * P * (t + 1)].bitcast(FP4X4),
                    lhsT_scale=w1s[:, P * t : P * (t + 1)],
                    rhs=xg[s0][:].bitcast(FP8X4),
                    rhs_scale=xgs[:, s0 : s0 + S_PART],
                    start=True,
                    stop=True,
                )
                nc.scalar.copy(y[t][:, s0 : s0 + S_PART], acc[:])

        w2 = keep.tile([P, 2 * N], U8, name="w2", align_bytes=64)
        w2s = keep.tile([P, N], U8, name="w2s", align_bytes=64)
        deal_words(nc, w2, w2_raw[:, : 2 * N])
        deal_scales(nc, w2s, w2_raw[:, 2 * N :])

        parts = range(0, V, V_PART)
        waves = [[(0, 0, V), (1, 0, V)], [(2, 0, V)] + [(3, v0, V_PART) for v0 in parts]]
        nd = {}
        r = {}
        for wave in waves:
            ya = {}
            for t in sorted(set(piece[0] for piece in wave)):
                ya[t] = keep.tile([P, V], F32, name=f"ya{t}", align_bytes=64)
                nc.vector.tensor_copy(ya[t][:], y[t][:].indirect(a_t[:]))
            stages = {}
            for piece in wave:
                t, v0, width = piece
                nd[piece] = keep.tile([P, width], F32, name=f"nd{t}_{v0}", align_bytes=64)
                nc.vector.tensor_tensor(
                    nd[piece][:],
                    y[t][:].indirect(b_t[:, v0 // LIST : (v0 + width) // LIST]),
                    ya[t][:, v0 : v0 + width],
                    ALU.subtract,
                )
                mag = keep.tile([P, width], F32, name=f"mag{t}_{v0}", align_bytes=64)
                sq = keep.tile([P, width], F32, name=f"sq{t}_{v0}", align_bytes=64)
                r[piece] = keep.tile([P, width], F32, name=f"r{t}_{v0}", align_bytes=64)
                stages[piece] = [
                    (mag, nd[piece], ACT.Abs, 0.0),
                    (sq, mag, ACT.Square, 0.25),
                    (r[piece], sq, ACT.Abs_reciprocal_sqrt, 0.0),
                ]
            for step in range(len(wave) + 2):
                for stage in range(3):
                    if 0 <= step - stage < len(wave):
                        dst, src, func, bias = stages[wave[step - stage]][stage]
                        nc.scalar.activation(dst[:], src[:], func, bias=bias)

        out_rows = out_0.rearrange("(p t) v -> p t v", t=PACK)
        out_words = out_1[0].rearrange("p c r -> p (c r)").bitcast(I32)
        oc = keep.tile([P, V], U32, name="oc", align_bytes=64)
        osc = keep.tile([P, V], U8, name="osc", align_bytes=64)
        zb = {v0: keep.tile([P, PACK, V_PART], BF16, name=f"zb{v0}", align_bytes=64) for v0 in parts}
        o32 = {}

        pull = {}

        def pull_of(piece):
            t, v0, width = piece
            pull[piece] = keep.tile([P, width], F32, name=f"pull{t}_{v0}", align_bytes=64)
            nc.vector.scalar_tensor_tensor(
                pull[piece][:], r[piece][:], gn_t[:, t : t + 1], rest_t[:, t, v0 : v0 + width], ALU.mult, ALU.mult
            )

        def force(piece, v0):
            t, first, width = piece
            cols = slice(v0 - first, v0 - first + V_PART)
            nc.vector.scalar_tensor_tensor(
                zb[v0][:, t, :], pull[piece][:, cols], gn_t[:, t : t + 1], nd[piece][:, cols], ALU.subtract, ALU.mult
            )

        for piece in waves[0]:
            pull_of(piece)
        for v0 in parts:
            for piece in waves[0]:
                force(piece, v0)
        pull_of(waves[1][0])
        for last in waves[1][1:]:
            v0 = last[1]
            pull_of(last)
            force(waves[1][0], v0)
            force(last, v0)
            zi = keep.tile([P, V_PART, PACK], BF16, name=f"zi{v0}", align_bytes=64)
            zc = keep.tile([P, V_PART], U32, name=f"zc{v0}", align_bytes=64)
            zs = keep.tile([P, V_PART], U8, name=f"zs{v0}", align_bytes=64)
            weave = nc.scalar.copy if v0 == 0 else nc.vector.tensor_copy
            weave(zi[:], zb[v0][:].rearrange("p t v -> p v t"))
            nc.vector.quantize_mx(out=zc[:].bitcast(FP8X4), scales=zs[:], in_=zi[:].rearrange("p v t -> p (v t)"))
            o32[v0] = keep.tile([P, PACK, V_PART], F32, name=f"o32{v0}", align_bytes=64)
            for t0 in range(0, PACK, 2):
                res = psum.tile([P, 2, V_PART], F32, name="res", tag="bank")
                for t in (t0, t0 + 1):
                    nc.tensor.matmul_mx(
                        out=res[:, t - t0, :],
                        lhsT=w2[:, 2 * P * t : 2 * P * (t + 1)].bitcast(FP4X4),
                        lhsT_scale=w2s[:, P * t : P * (t + 1)],
                        rhs=zc[:].bitcast(FP8X4),
                        rhs_scale=zs[:],
                        start=True,
                        stop=True,
                    )
                nc.scalar.copy(o32[v0][:, t0 : t0 + 2, :], res[:])
            nc.sync.dma_start(out=out_rows[:, :, v0 : v0 + V_PART], in_=o32[v0][:])
        for v0 in parts:
            oi = keep.tile([P, V_PART, PACK], BF16, name=f"oi{v0}", align_bytes=64)
            nc.vector.tensor_copy(out=oi[:], in_=o32[v0][:].rearrange("p t v -> p v t"))
            nc.vector.quantize_mx(
                out=oc[:, v0 : v0 + V_PART].bitcast(FP8X4),
                scales=osc[:, v0 : v0 + V_PART],
                in_=oi[:].rearrange("p v t -> p (v t)"),
            )
            nc.sync.dma_start(out=out_words[:, v0 : v0 + V_PART], in_=oc[:, v0 : v0 + V_PART].bitcast(I32))
        for q in range(4):
            queue = nc.scalar if q % 2 else nc.sync
            queue.dma_start(
                out=out_2[0].bitcast(I32)[4 * q : 4 * q + 4, :], in_=osc[:].bitcast(I32)[32 * q : 32 * q + 4, :]
            )
